import numpy as np
import ml_dtypes


def mxq(x, axis, fmt="e4m3"):
    dtype, down = {"e4m3": (ml_dtypes.float8_e4m3fn, 7), "e5m2": (ml_dtypes.float8_e5m2, 14)}[fmt]
    v = np.moveaxis(np.asarray(x, np.float32).astype(ml_dtypes.bfloat16).astype(np.float64), axis, -1)
    blocks = v.reshape(v.shape[:-1] + (-1, 32))
    amax = np.abs(blocks).max(-1, keepdims=True)
    byte = np.maximum(np.where(amax > 0, np.frexp(amax)[1] - 1 + 127, 0) - down, 1)
    scale = np.exp2(byte - 127.0)
    codes = (blocks / scale).astype(np.float32).astype(dtype).astype(np.float64)
    return np.moveaxis((codes * scale).reshape(v.shape), -1, axis)


WIDE = False


def mx_kscale(k, group=512):
    if not WIDE:
        return np.ones(k)
    levels = np.array([10, -10, 5, -5, 0])
    if group != 512:
        return np.exp2(np.random.permutation(np.resize(levels, k // group))).repeat(group)
    if k % 512:
        return np.exp2(np.random.permutation(np.resize(levels, k // 32))).repeat(32)
    a = np.empty((k // 512, 16))
    for p in range(k // 512):
        a[p, :8] = np.random.permutation(np.resize(levels, 8))
        for g in range(8):
            far = levels[np.abs(levels - a[p, g]) >= 10]
            a[p, g + 8] = far[np.random.randint(len(far))]
    return np.exp2(a.ravel()).repeat(32)


def f64(x):
    return np.asarray(x).astype(np.float64)


G, D, M, O, N = 2, 256, 256, 256, 512


def sgn(shape):
    return np.random.uniform(0.5, 2.0, shape) * np.where(np.random.standard_normal(shape) < 0, -1.0, 1.0)


def setup_inputs():
    n = np.random.standard_normal
    s_d = mx_kscale(D, 0)
    s_m = mx_kscale(M, 0)
    return {
        "x": (n((G, D, N)) * s_d[:, None]).astype(np.float32),
        "w1": (n((G, D, M)) / np.sqrt(D) / s_d[:, None]).astype(np.float32),
        "w2": (n((G, D, M)) / np.sqrt(D) / s_d[:, None]).astype(np.float32),
        "hs": (sgn((G, M, 1)) * s_m[:, None]).astype(np.float32),
        "wo2": (n((G, M, O)) / np.sqrt(M) / s_m[:, None]).astype(np.float32),
        "ob": (0.5 * n((G, O, 1))).astype(np.float32),
        "osc": (np.random.uniform(0.5, 2.0, (G, O, 1))).astype(np.float32),
    }


def reference(x, w1, w2, hs, wo2, ob, osc):
    w1q = mxq(f64(w1), 1, "e4m3")
    xq = mxq(f64(x), 1, "e4m3")
    z1 = w1q.transpose(0, 2, 1) @ xq
    w2q = mxq(f64(w2), 1, "e4m3")
    z2 = w2q.transpose(0, 2, 1) @ xq
    pr = z1 * z2
    mu = np.mean(pr, axis=-1, keepdims=True)
    ms = np.sqrt(np.mean(np.square(z1), axis=-1, keepdims=True) + 0.1)
    h = (pr - mu) / ms
    hh = h * f64(hs)
    wo2q = mxq(f64(wo2), 1, "e4m3")
    hhq = mxq(hh, 1, "e4m3")
    y0 = wo2q.transpose(0, 2, 1) @ hhq
    y = np.tanh(y0 + f64(ob)) * f64(osc)
    return y

@@ -1,0 +1,210 @@
+from contextlib import ExitStack
+
+import concourse.mybir as mybir
+
+G, D, M, O, N = 2, 256, 256, 256, 512
+FLOPS = 2 * G * N * (2 * D * M + M * O)
+
+F32 = mybir.dt.float32
+BF16 = mybir.dt.bfloat16
+I32 = mybir.dt.int32
+U32 = mybir.dt.uint32
+U8 = mybir.dt.uint8
+FP8X4 = mybir.dt.float8_e4m3fn_x4
+ACT = mybir.ActivationFunctionType
+ALU = mybir.AluOpType
+
+P = 128
+R = 64
+PACK = 4
+EPS = 0.1
+X_SPLIT = 352
+
+
+def tile_rows_frowcorr_kernel(tc, x, w1, w2, hs, wo2, ob, osc, out):
+    nc = tc.nc
+    with ExitStack() as ctx:
+        sb = ctx.enter_context(tc.tile_pool(name="sb", bufs=1))
+        ps = ctx.enter_context(tc.psum_pool(name="ps", bufs=1))
+        ctx.enter_context(tc.manual_schedule())
+
+        def sbuf(name, shape, dtype):
+            return sb.tile(shape, dtype, name=name, align_bytes=64)
+
+        def rows(g):
+            return slice(R * g, R * (g + 1))
+
+        def load_rows(name, src):
+            width = src.shape[2]
+            raw = sbuf(name, [P, PACK, width], F32)
+            nc.sync.dma_start(out=raw[:], in_=src.rearrange("g (p j) c -> (g p) j c", j=PACK))
+            return raw
+
+        def quantize(name, words, parts):
+            width = words.shape[1]
+            codes = sbuf(name + "_codes", [P, width], U32)
+            scales = sbuf(name + "_scales", [P, width], U8)
+            nc.vector.quantize_mx(
+                out=codes[0:parts, :].bitcast(FP8X4),
+                scales=scales[0:parts, :],
+                in_=words[0:parts].rearrange("q c j -> q (c j)"),
+            )
+            return codes, scales
+
+        def product(bank, g, stat, t, mov):
+            cols = slice(P * t, P * (t + 1))
+            nc.tensor.matmul_mx(
+                out=bank[:],
+                lhsT=stat[0][rows(g), cols].bitcast(FP8X4),
+                lhsT_scale=stat[1][rows(g), cols],
+                rhs=mov[0][rows(g), :].bitcast(FP8X4),
+                rhs_scale=mov[1][rows(g), :],
+                start=True,
+                stop=True,
+            )
+
+        x_raw = load_rows("x_raw", x)
+        w1_raw = load_rows("w1_raw", w1)
+        w2_raw = load_rows("w2_raw", w2)
+        hs_sb = sbuf("hs_sb", [P, G, 2], F32)
+        hs_v = hs.rearrange("g (p h t) one -> h p g (t one)", h=2, t=2)
+        for h in range(2):
+            nc.sync.dma_start(out=hs_sb[rows(h)], in_=hs_v[h])
+        wo_raw = load_rows("wo_raw", wo2)
+        ob_sb = sbuf("ob_sb", [P, G, 2], F32)
+        nc.sync.dma_start(out=ob_sb[:], in_=ob.rearrange("g (q t) one -> q g (t one)", t=2))
+        osc_sb = sbuf("osc_sb", [P, G, 2], F32)
+        nc.sync.dma_start(out=osc_sb[:], in_=osc.rearrange("g (q t) one -> q g (t one)", t=2))
+
+        warm = sbuf("warm", [P, 2], F32)
+        nc.vector.memset(warm[:, 0:1], 1.0)
+        nc.scalar.activation(out=warm[:, 1:2], in_=warm[:, 0:1], func=ACT.Abs_reciprocal_sqrt)
+
+        x_words = sbuf("x_words", [P, N, PACK], BF16)
+        x_dst = x_words[:].rearrange("q (c i) j -> q c j i", i=4)
+        x_src = x_raw[:].rearrange("q j (c i) -> q c j i", i=4)
+        cs = X_SPLIT // 4
+        nc.vector.tensor_copy(out=x_dst[:, 0:cs], in_=x_src[:, 0:cs])
+        nc.scalar.copy(out=x_dst[:, cs:], in_=x_src[:, cs:])
+        xq = quantize("x", x_words, P)
+
+        def deal(name, raw):
+            words = sbuf(name + "_words", [P, M, PACK], BF16)
+            dst = words[:].rearrange("q (t h p) j -> q p h t j", t=2, h=2)
+            src = raw[:].rearrange("q j (p h t) -> q p h t j", t=2, h=2)
+            nc.scalar.copy(out=dst[:, 32:], in_=src[:, 32:])
+            nc.vector.tensor_copy(out=dst[:, 0:32], in_=src[:, 0:32])
+            return quantize(name, words, P)
+
+        z1 = [[ps.tile([P, N], F32, name="z1_%d%d" % (g, t)) for t in range(2)] for g in range(G)]
+        z2 = [[ps.tile([P, N], F32, name="z2_%d%d" % (g, t)) for t in range(2)] for g in range(G)]
+
+        w1q = deal("w1", w1_raw)
+        for t in range(2):
+            product(z1[0][t], 0, w1q, t, xq)
+        w2q = deal("w2", w2_raw)
+        for t in range(2):
+            product(z2[0][t], 0, w2q, t, xq)
+            product(z1[1][t], 1, w1q, t, xq)
+        for t in range(2):
+            product(z2[1][t], 1, w2q, t, xq)
+
+        wo_words = sbuf("wo_words", [P, O, PACK], BF16)
+        for t in range(2):
+            nc.gpsimd.tensor_scalar(
+                out=wo_words[:, P * t : P * (t + 1), :],
+                in0=wo_raw[:].rearrange("q j (p t) -> q t p j", t=2)[:, t],
+                scalar1=1.0, scalar2=0.0, op0=ALU.mult, op1=ALU.add,
+            )
+
+        squares = sbuf("squares", [P, N], BF16)
+        pairs = []
+        for g in range(G):
+            sumsq = sbuf("sumsq%d" % g, [P, 2], F32)
+            rs = sbuf("rs%d" % g, [P, 2], F32)
+            sumpr = sbuf("sumpr%d" % g, [P, 2], F32)
+            mu = sbuf("mu%d" % g, [P, 2], F32)
+            fac = sbuf("fac%d" % g, [P, 2], F32)
+            pr = []
+            z1_sb = []
+            for t in range(2):
+                cp = sbuf("z1_sb%d%d" % (g, t), [P, N], F32)
+                if g == 0 and t == 1:
+                    nc.vector.tensor_copy(out=cp[:], in_=z1[g][t][:])
+                else:
+                    nc.scalar.copy(out=cp[:], in_=z1[g][t][:])
+                z1_sb.append(cp)
+            for t in range(2):
+                prt = sbuf("pr%d%d" % (g, t), [P, N], F32)
+                nc.vector.scalar_tensor_tensor(
+                    out=prt[:], in0=z2[g][t][:], scalar=1.0, in1=z1_sb[t][:],
+                    op0=ALU.mult, op1=ALU.mult, accum_out=sumpr[:, t : t + 1],
+                )
+                pr.append(prt)
+            for t in range(2):
+                nc.scalar.activation(
+                    out=squares[:], in_=z1[g][t][:], func=ACT.Square, accum_out=sumsq[:, t : t + 1]
+                )
+            nc.scalar.activation(
+                out=rs[:], in_=sumsq[:], func=ACT.Abs_reciprocal_sqrt, scale=1.0 / N, bias=EPS
+            )
+            nc.vector.tensor_tensor(out=fac[:], in0=rs[:], in1=hs_sb[:, g, :], op=ALU.mult)
+            nc.vector.tensor_scalar(
+                out=mu[:], in0=sumpr[:], scalar1=1.0 / N, scalar2=None, op0=ALU.mult
+            )
+            chunks = g + 1
+            width = N // chunks
+            pws = []
+            for c in range(chunks):
+                pair = sbuf("pair%d%d" % (g, c), [P, 2, width, 2], BF16)
+                for t in range(2):
+                    nc.vector.tensor_scalar(
+                        out=pair[:, g, :, t], in0=pr[t][:, c * width : (c + 1) * width],
+                        scalar1=mu[:, t : t + 1],
+                        scalar2=fac[:, t : t + 1], op0=ALU.subtract, op1=ALU.mult,
+                    )
+                pw = pair[:].rearrange("q h n t -> q h (n t)").bitcast(I32)
+                nc.sync.dma_start(out=pw[rows(g), 1 - g, :], in_=pw[rows(1 - g), g, :])
+                pws.append(pw)
+            pairs.append(pws)
+
+        nc.scalar.activation(out=warm[:, 1:2], in_=warm[:, 0:1], func=ACT.Tanh)
+
+        woq = quantize("wo", wo_words, P)
+        h_words = sbuf("h_words", [P, N, PACK], BF16)
+        hw = h_words[:].rearrange("q n j -> q (n j)").bitcast(I32)
+        out_v = out.rearrange("g (q t) n -> g t q n", t=2)
+        for g in range(G):
+            chunks = g + 1
+            width = N // chunks
+            parts = R * (g + 1)
+            codes = sbuf("h_codes%d" % g, [P, N], U32)
+            scales = sbuf("h_scales%d" % g, [P, N], U8)
+            for c in range(chunks):
+                cols = slice(c * width, (c + 1) * width)
+                nc.vector.tensor_copy(
+                    out=hw[rows(g), 2 * c * width : 2 * (c + 1) * width].rearrange("q (c i h) -> q c h i", i=4, h=2),
+                    in_=pairs[g][c][rows(g)].rearrange("q h (c i) -> q c h i", i=4),
+                )
+                nc.vector.quantize_mx(
+                    out=codes[0:parts, cols].bitcast(FP8X4),
+                    scales=scales[0:parts, cols],
+                    in_=h_words[0:parts, cols, :].rearrange("q c j -> q (c j)"),
+                )
+            for t in range(2):
+                product(z1[g][t], g, woq, t, (codes, scales))
+        for g in range(G):
+            for t in range(2):
+                chunks = 2 if (g, t) == (1, 1) else 1
+                width = N // chunks
+                for c in range(chunks):
+                    cols = slice(c * width, (c + 1) * width)
+                    th = sbuf("th%d%d%d" % (g, t, c), [P, width], F32)
+                    nc.scalar.activation(
+                        out=th[:], in_=z1[g][t][:, cols], func=ACT.Tanh, bias=ob_sb[:, g, t : t + 1]
+                    )
+                    res = sbuf("res%d%d%d" % (g, t, c), [P, width], F32)
+                    nc.vector.tensor_scalar(
+                        out=res[:], in0=th[:], scalar1=osc_sb[:, g, t : t + 1], scalar2=None, op0=ALU.mult
+                    )
+                    nc.sync.dma_start(out=out_v[g, t][:, cols], in_=res[:])

@@ -51,12 +51,11 @@ def tile_rows_frowcorr_kernel(tc, x, w1, w2, hs, wo2, ob, osc, out):
             )
             return codes, scales
 
-        def product(bank, g, stat, t, mov):
-            cols = slice(P * t, P * (t + 1))
+        def product(bank, g, stat, mov):
             nc.tensor.matmul_mx(
                 out=bank[:],
-                lhsT=stat[0][rows(g), cols].bitcast(FP8X4),
-                lhsT_scale=stat[1][rows(g), cols],
+                lhsT=stat[0][rows(g), :].bitcast(FP8X4),
+                lhsT_scale=stat[1][rows(g), :],
                 rhs=mov[0][rows(g), :].bitcast(FP8X4),
                 rhs_scale=mov[1][rows(g), :],
                 start=True,
@@ -66,11 +65,11 @@ def tile_rows_frowcorr_kernel(tc, x, w1, w2, hs, wo2, ob, osc, out):
         x_raw = load_rows("x_raw", x)
         w1_raw = load_rows("w1_raw", w1)
         w2_raw = load_rows("w2_raw", w2)
+        wo_raw = load_rows("wo_raw", wo2)
         hs_sb = sbuf("hs_sb", [P, G, 2], F32)
         hs_v = hs.rearrange("g (p h t) one -> h p g (t one)", h=2, t=2)
         for h in range(2):
             nc.sync.dma_start(out=hs_sb[rows(h)], in_=hs_v[h])
-        wo_raw = load_rows("wo_raw", wo2)
         ob_sb = sbuf("ob_sb", [P, G, 2], F32)
         nc.sync.dma_start(out=ob_sb[:], in_=ob.rearrange("g (q t) one -> q g (t one)", t=2))
         osc_sb = sbuf("osc_sb", [P, G, 2], F32)
@@ -84,30 +83,46 @@ def tile_rows_frowcorr_kernel(tc, x, w1, w2, hs, wo2, ob, osc, out):
         x_dst = x_words[:].rearrange("q (c i) j -> q c j i", i=4)
         x_src = x_raw[:].rearrange("q j (c i) -> q c j i", i=4)
         cs = X_SPLIT // 4
-        nc.vector.tensor_copy(out=x_dst[:, 0:cs], in_=x_src[:, 0:cs])
+        ch = N // 8
+        nc.vector.tensor_copy(out=x_dst[:, 0:ch], in_=x_src[:, 0:ch])
+        nc.vector.tensor_copy(out=x_dst[:, ch:cs], in_=x_src[:, ch:cs])
         nc.scalar.copy(out=x_dst[:, cs:], in_=x_src[:, cs:])
-        xq = quantize("x", x_words, P)
+        xq = (sbuf("x_codes", [P, N], U32), sbuf("x_scales", [P, N], U8))
+        for c in range(2):
+            cols = slice(c * (N // 2), (c + 1) * (N // 2))
+            nc.vector.quantize_mx(
+                out=xq[0][:, cols].bitcast(FP8X4),
+                scales=xq[1][:, cols],
+                in_=x_words[:, cols, :].rearrange("q c j -> q (c j)"),
+            )
 
-        def deal(name, raw):
-            words = sbuf(name + "_words", [P, M, PACK], BF16)
-            dst = words[:].rearrange("q (t h p) j -> q p h t j", t=2, h=2)
-            src = raw[:].rearrange("q j (p h t) -> q p h t j", t=2, h=2)
-            nc.scalar.copy(out=dst[:, 32:], in_=src[:, 32:])
-            nc.vector.tensor_copy(out=dst[:, 0:32], in_=src[:, 0:32])
-            return quantize(name, words, P)
+        def deal(name, raw, t, copy):
+            words = sbuf(name + "_words", [P, P, PACK], BF16)
+            copy(
+                out=words[:].rearrange("q (h p) j -> q p h j", h=2),
+                in_=raw[:].rearrange("q j (p h t) -> q t p h j", t=2, h=2)[:, t],
+            )
+            return words
 
         z1 = [[ps.tile([P, N], F32, name="z1_%d%d" % (g, t)) for t in range(2)] for g in range(G)]
         z2 = [[ps.tile([P, N], F32, name="z2_%d%d" % (g, t)) for t in range(2)] for g in range(G)]
 
-        w1q = deal("w1", w1_raw)
-        for t in range(2):
-            product(z1[0][t], 0, w1q, t, xq)
-        w2q = deal("w2", w2_raw)
-        for t in range(2):
-            product(z2[0][t], 0, w2q, t, xq)
-            product(z1[1][t], 1, w1q, t, xq)
-        for t in range(2):
-            product(z2[1][t], 1, w2q, t, xq)
+        w10 = deal("w10", w1_raw, 0, nc.scalar.copy)
+        w11 = deal("w11", w1_raw, 1, nc.vector.tensor_copy)
+        w1q0 = quantize("w10", w10, P)
+        product(z1[0][0], 0, w1q0, xq)
+        product(z1[1][0], 1, w1q0, xq)
+        w20 = deal("w20", w2_raw, 0, nc.vector.tensor_copy)
+        w21 = deal("w21", w2_raw, 1, nc.scalar.copy)
+        w1q1 = quantize("w11", w11, P)
+        w2q0 = quantize("w20", w20, P)
+        w2q1 = quantize("w21", w21, P)
+        product(z2[0][0], 0, w2q0, xq)
+        product(z1[0][1], 0, w1q1, xq)
+        product(z2[1][0], 1, w2q0, xq)
+        product(z2[0][1], 0, w2q1, xq)
+        product(z1[1][1], 1, w1q1, xq)
+        product(z2[1][1], 1, w2q1, xq)
 
         wo_words = sbuf("wo_words", [P, O, PACK], BF16)
         for t in range(2):
@@ -118,81 +133,113 @@ def tile_rows_frowcorr_kernel(tc, x, w1, w2, hs, wo2, ob, osc, out):
             )
 
         squares = sbuf("squares", [P, N], BF16)
-        pairs = []
-        for g in range(G):
-            sumsq = sbuf("sumsq%d" % g, [P, 2], F32)
-            rs = sbuf("rs%d" % g, [P, 2], F32)
-            sumpr = sbuf("sumpr%d" % g, [P, 2], F32)
-            mu = sbuf("mu%d" % g, [P, 2], F32)
-            fac = sbuf("fac%d" % g, [P, 2], F32)
-            pr = []
-            z1_sb = []
-            for t in range(2):
-                cp = sbuf("z1_sb%d%d" % (g, t), [P, N], F32)
-                if g == 0 and t == 1:
-                    nc.vector.tensor_copy(out=cp[:], in_=z1[g][t][:])
-                else:
-                    nc.scalar.copy(out=cp[:], in_=z1[g][t][:])
-                z1_sb.append(cp)
-            for t in range(2):
-                prt = sbuf("pr%d%d" % (g, t), [P, N], F32)
-                nc.vector.scalar_tensor_tensor(
-                    out=prt[:], in0=z2[g][t][:], scalar=1.0, in1=z1_sb[t][:],
-                    op0=ALU.mult, op1=ALU.mult, accum_out=sumpr[:, t : t + 1],
-                )
-                pr.append(prt)
-            for t in range(2):
-                nc.scalar.activation(
-                    out=squares[:], in_=z1[g][t][:], func=ACT.Square, accum_out=sumsq[:, t : t + 1]
-                )
+        sumsq = [sbuf("sumsq%d" % g, [P, 2], F32) for g in range(G)]
+        rs = [sbuf("rs%d" % g, [P, 2], F32) for g in range(G)]
+        fac = [sbuf("fac%d" % g, [P, 2], F32) for g in range(G)]
+        sumpr = [[sbuf("sumpr%d%d" % (g, t), [P, 1], F32) for t in range(2)] for g in range(G)]
+        mu = [[sbuf("mu%d%d" % (g, t), [P, 1], F32) for t in range(2)] for g in range(G)]
+        z1_sb = [[sbuf("z1_sb%d%d" % (g, t), [P, N], F32) for t in range(2)] for g in range(G)]
+        pr = [[sbuf("pr%d%d" % (g, t), [P, N], F32) for t in range(2)] for g in range(G)]
+
+        def square(g, t):
             nc.scalar.activation(
-                out=rs[:], in_=sumsq[:], func=ACT.Abs_reciprocal_sqrt, scale=1.0 / N, bias=EPS
+                out=squares[:], in_=z1[g][t][:], func=ACT.Square, accum_out=sumsq[g][:, t : t + 1]
             )
-            nc.vector.tensor_tensor(out=fac[:], in0=rs[:], in1=hs_sb[:, g, :], op=ALU.mult)
+
+        def root(g):
+            nc.scalar.activation(
+                out=rs[g][:], in_=sumsq[g][:], func=ACT.Abs_reciprocal_sqrt, scale=1.0 / N, bias=EPS
+            )
+
+        def multiply(g, t):
+            nc.vector.scalar_tensor_tensor(
+                out=pr[g][t][:], in0=z2[g][t][:], scalar=1.0, in1=z1_sb[g][t][:],
+                op0=ALU.mult, op1=ALU.mult, accum_out=sumpr[g][t][:],
+            )
+
+        def mean(g, t):
             nc.vector.tensor_scalar(
-                out=mu[:], in0=sumpr[:], scalar1=1.0 / N, scalar2=None, op0=ALU.mult
+                out=mu[g][t][:], in0=sumpr[g][t][:], scalar1=1.0 / N, scalar2=None, op0=ALU.mult
             )
-            chunks = g + 1
-            width = N // chunks
-            pws = []
-            for c in range(chunks):
-                pair = sbuf("pair%d%d" % (g, c), [P, 2, width, 2], BF16)
-                for t in range(2):
-                    nc.vector.tensor_scalar(
-                        out=pair[:, g, :, t], in0=pr[t][:, c * width : (c + 1) * width],
-                        scalar1=mu[:, t : t + 1],
-                        scalar2=fac[:, t : t + 1], op0=ALU.subtract, op1=ALU.mult,
-                    )
-                pw = pair[:].rearrange("q h n t -> q h (n t)").bitcast(I32)
-                nc.sync.dma_start(out=pw[rows(g), 1 - g, :], in_=pw[rows(1 - g), g, :])
-                pws.append(pw)
-            pairs.append(pws)
+
+        def factor(g):
+            nc.vector.tensor_tensor(out=fac[g][:], in0=rs[g][:], in1=hs_sb[:, g, :], op=ALU.mult)
+
+        def centre(g, t, pair, cols):
+            nc.vector.tensor_scalar(
+                out=pair[:, g, :, t], in0=pr[g][t][:, cols], scalar1=mu[g][t][:],
+                scalar2=fac[g][:, t : t + 1], op0=ALU.subtract, op1=ALU.mult,
+            )
+
+        def swap(g, pair):
+            pw = pair[:].rearrange("q h n t -> q h (n t)").bitcast(I32)
+            nc.sync.dma_start(out=pw[rows(g), 1 - g, :], in_=pw[rows(1 - g), g, :])
+            return pw
+
+        H = N // 2
+        halves = [slice(0, H), slice(H, N)]
+        pair0 = sbuf("pair0", [P, 2, N, 2], BF16)
+        pair1 = [sbuf("pair1%d" % c, [P, 2, H, 2], BF16) for c in range(2)]
+
+        nc.scalar.copy(out=z1_sb[0][0][:], in_=z1[0][0][:])
+        nc.vector.tensor_copy(out=z1_sb[1][0][:], in_=z1[1][0][:])
+        square(0, 0)
+        multiply(0, 0)
+        nc.scalar.copy(out=z1_sb[0][1][:], in_=z1[0][1][:])
+        square(0, 1)
+        root(0)
+        multiply(1, 0)
+        mean(0, 0)
+        multiply(0, 1)
+        mean(1, 0)
+        factor(0)
+        mean(0, 1)
+        centre(0, 0, pair0, slice(0, N))
+        centre(0, 1, pair0, slice(0, N))
+        pw0 = swap(0, pair0)
+        nc.scalar.copy(out=z1_sb[1][1][:], in_=z1[1][1][:])
+        square(1, 0)
+        square(1, 1)
+        root(1)
+        multiply(1, 1)
+        factor(1)
+        mean(1, 1)
+        pw1 = []
+        for c in range(2):
+            for t in range(2):
+                centre(1, t, pair1[c], halves[c])
+            pw1.append(swap(1, pair1[c]))
 
         nc.scalar.activation(out=warm[:, 1:2], in_=warm[:, 0:1], func=ACT.Tanh)
 
-        woq = quantize("wo", wo_words, P)
         h_words = sbuf("h_words", [P, N, PACK], BF16)
         hw = h_words[:].rearrange("q n j -> q (n j)").bitcast(I32)
         out_v = out.rearrange("g (q t) n -> g t q n", t=2)
-        for g in range(G):
-            chunks = g + 1
-            width = N // chunks
-            parts = R * (g + 1)
-            codes = sbuf("h_codes%d" % g, [P, N], U32)
-            scales = sbuf("h_scales%d" % g, [P, N], U8)
-            for c in range(chunks):
-                cols = slice(c * width, (c + 1) * width)
-                nc.vector.tensor_copy(
-                    out=hw[rows(g), 2 * c * width : 2 * (c + 1) * width].rearrange("q (c i h) -> q c h i", i=4, h=2),
-                    in_=pairs[g][c][rows(g)].rearrange("q h (c i) -> q c h i", i=4),
-                )
-                nc.vector.quantize_mx(
-                    out=codes[0:parts, cols].bitcast(FP8X4),
-                    scales=scales[0:parts, cols],
-                    in_=h_words[0:parts, cols, :].rearrange("q c j -> q (c j)"),
-                )
-            for t in range(2):
-                product(z1[g][t], g, woq, t, (codes, scales))
+
+        def join(g, pw, cols):
+            nc.vector.tensor_copy(
+                out=hw[rows(g), 2 * cols.start : 2 * cols.stop].rearrange("q (c i h) -> q c h i", i=4, h=2),
+                in_=pw[rows(g)].rearrange("q h (c i) -> q c h i", i=4),
+            )
+
+        join(0, pw0, slice(0, N))
+        wo_codes, wo_scales = quantize("wo", wo_words, P)
+        woq = [(wo_codes[:, P * t : P * (t + 1)], wo_scales[:, P * t : P * (t + 1)]) for t in range(2)]
+        hq0 = quantize("h0", h_words, R)
+        for t in range(2):
+            product(z1[0][t], 0, woq[t], hq0)
+        h1_codes = sbuf("h1_codes", [P, N], U32)
+        h1_scales = sbuf("h1_scales", [P, N], U8)
+        for c in range(2):
+            join(1, pw1[c], halves[c])
+        for c in range(2):
+            nc.vector.quantize_mx(
+                out=h1_codes[:, halves[c]].bitcast(FP8X4),
+                scales=h1_scales[:, halves[c]],
+                in_=h_words[:, halves[c], :].rearrange("q c j -> q (c j)"),
+            )
+        for t in range(2):
+            product(z1[1][t], 1, woq[t], (h1_codes, h1_scales))
         for g in range(G):
             for t in range(2):
                 chunks = 2 if (g, t) == (1, 1) else 1

@@ -124,13 +124,6 @@ def tile_rows_frowcorr_kernel(tc, x, w1, w2, hs, wo2, ob, osc, out):
         product(z1[1][1], 1, w1q1, xq)
         product(z2[1][1], 1, w2q1, xq)
 
-        wo_words = sbuf("wo_words", [P, O, PACK], BF16)
-        for t in range(2):
-            nc.gpsimd.tensor_scalar(
-                out=wo_words[:, P * t : P * (t + 1), :],
-                in0=wo_raw[:].rearrange("q j (p t) -> q t p j", t=2)[:, t],
-                scalar1=1.0, scalar2=0.0, op0=ALU.mult, op1=ALU.add,
-            )
 
         squares = sbuf("squares", [P, N], BF16)
         sumsq = [sbuf("sumsq%d" % g, [P, 2], F32) for g in range(G)]
@@ -209,6 +202,12 @@ def tile_rows_frowcorr_kernel(tc, x, w1, w2, hs, wo2, ob, osc, out):
             for t in range(2):
                 centre(1, t, pair1[c], halves[c])
             pw1.append(swap(1, pair1[c]))
+
+        wo_words = sbuf("wo_words", [P, O, PACK], BF16)
+        nc.scalar.copy(
+            out=wo_words[:].rearrange("q (t p) j -> q p t j", t=2),
+            in_=wo_raw[:].rearrange("q j (p t) -> q p t j", t=2),
+        )
 
         nc.scalar.activation(out=warm[:, 1:2], in_=warm[:, 0:1], func=ACT.Tanh)
 

@@ -79,6 +79,28 @@ def tile_rows_frowcorr_kernel(tc, x, w1, w2, hs, wo2, ob, osc, out):
         nc.vector.memset(warm[:, 0:1], 1.0)
         nc.scalar.activation(out=warm[:, 1:2], in_=warm[:, 0:1], func=ACT.Abs_reciprocal_sqrt)
 
+        ones = sbuf("ones", [P, P * PACK], BF16)
+        nc.vector.memset(ones[:].bitcast(I32), 0x3F803F80)
+        onesq = (sbuf("ones_codes", [P, N], U32), sbuf("ones_scales", [P, N], U8))
+        for c in range(N // P):
+            cols = slice(c * P, (c + 1) * P)
+            nc.vector.quantize_mx(out=onesq[0][:, cols].bitcast(FP8X4), scales=onesq[1][:, cols], in_=ones[:])
+        idle_bank = ps.tile([P, N], F32, name="idle_bank")
+
+        def keep_warm(count, stat):
+            for k in range(count):
+                nc.tensor.matmul_mx(
+                    out=idle_bank[:],
+                    lhsT=stat[0][:, 0:P].bitcast(FP8X4),
+                    lhsT_scale=stat[1][:, 0:P],
+                    rhs=onesq[0][:].bitcast(FP8X4),
+                    rhs_scale=onesq[1][:],
+                    start=True,
+                    stop=True,
+                )
+
+        keep_warm(12, onesq)
+
         x_words = sbuf("x_words", [P, N, PACK], BF16)
         x_dst = x_words[:].rearrange("q (c i) j -> q c j i", i=4)
         x_src = x_raw[:].rearrange("q j (c i) -> q c j i", i=4)
@@ -96,6 +118,8 @@ def tile_rows_frowcorr_kernel(tc, x, w1, w2, hs, wo2, ob, osc, out):
                 in_=x_words[:, cols, :].rearrange("q c j -> q (c j)"),
             )
 
+        keep_warm(1, xq)
+
         def deal(name, raw, t, copy):
             words = sbuf(name + "_words", [P, P, PACK], BF16)
             copy(
@@ -105,7 +129,8 @@ def tile_rows_frowcorr_kernel(tc, x, w1, w2, hs, wo2, ob, osc, out):
             return words
 
         z1 = [[ps.tile([P, N], F32, name="z1_%d%d" % (g, t)) for t in range(2)] for g in range(G)]
-        z2 = [[ps.tile([P, N], F32, name="z2_%d%d" % (g, t)) for t in range(2)] for g in range(G)]
+        z2_1 = ps.tile([P, N], F32, name="z2_1")
+        z2 = [[ps.tile([P, N], F32, name="z2_0%d" % t) for t in range(2)], [z2_1, z2_1]]
 
         w10 = deal("w10", w1_raw, 0, nc.scalar.copy)
         w11 = deal("w11", w1_raw, 1, nc.vector.tensor_copy)
@@ -122,7 +147,6 @@ def tile_rows_frowcorr_kernel(tc, x, w1, w2, hs, wo2, ob, osc, out):
         product(z2[1][0], 1, w2q0, xq)
         product(z2[0][1], 0, w2q1, xq)
         product(z1[1][1], 1, w1q1, xq)
-        product(z2[1][1], 1, w2q1, xq)
 
 
         squares = sbuf("squares", [P, N], BF16)
@@ -182,8 +206,11 @@ def tile_rows_frowcorr_kernel(tc, x, w1, w2, hs, wo2, ob, osc, out):
         square(0, 1)
         root(0)
         multiply(1, 0)
+        product(z2[1][1], 1, w2q1, xq)
         mean(0, 0)
         multiply(0, 1)
+        product(z2[0][1], 0, w2q1, xq)
+        keep_warm(3, onesq)
         mean(1, 0)
         factor(0)
         mean(0, 1)
@@ -195,6 +222,8 @@ def tile_rows_frowcorr_kernel(tc, x, w1, w2, hs, wo2, ob, osc, out):
         square(1, 1)
         root(1)
         multiply(1, 1)
+        product(z2[1][1], 1, w2q1, xq)
+        keep_warm(6, onesq)
         factor(1)
         mean(1, 1)
         pw1 = []
@@ -224,9 +253,11 @@ def tile_rows_frowcorr_kernel(tc, x, w1, w2, hs, wo2, ob, osc, out):
         join(0, pw0, slice(0, N))
         wo_codes, wo_scales = quantize("wo", wo_words, P)
         woq = [(wo_codes[:, P * t : P * (t + 1)], wo_scales[:, P * t : P * (t + 1)]) for t in range(2)]
+        keep_warm(2, (wo_codes, wo_scales))
         hq0 = quantize("h0", h_words, R)
         for t in range(2):
             product(z1[0][t], 0, woq[t], hq0)
+        keep_warm(2, onesq)
         h1_codes = sbuf("h1_codes", [P, N], U32)
         h1_scales = sbuf("h1_scales", [P, N], U8)
         for c in range(2):

from contextlib import ExitStack

import concourse.mybir as mybir

G, D, M, O, N = 2, 256, 256, 256, 512
FLOPS = 2 * G * N * (2 * D * M + M * O)

F32 = mybir.dt.float32
BF16 = mybir.dt.bfloat16
I32 = mybir.dt.int32
U32 = mybir.dt.uint32
U8 = mybir.dt.uint8
FP8X4 = mybir.dt.float8_e4m3fn_x4
ACT = mybir.ActivationFunctionType
ALU = mybir.AluOpType

P = 128
R = 64
PACK = 4
EPS = 0.1
X_SPLIT = 352


def tile_rows_frowcorr_kernel(tc, x, w1, w2, hs, wo2, ob, osc, out):
    nc = tc.nc
    with ExitStack() as ctx:
        sb = ctx.enter_context(tc.tile_pool(name="sb", bufs=1))
        ps = ctx.enter_context(tc.psum_pool(name="ps", bufs=1))
        ctx.enter_context(tc.manual_schedule())

        def sbuf(name, shape, dtype):
            return sb.tile(shape, dtype, name=name, align_bytes=64)

        def rows(g):
            return slice(R * g, R * (g + 1))

        def load_rows(name, src):
            width = src.shape[2]
            raw = sbuf(name, [P, PACK, width], F32)
            nc.sync.dma_start(out=raw[:], in_=src.rearrange("g (p j) c -> (g p) j c", j=PACK))
            return raw

        def quantize(name, words, parts):
            width = words.shape[1]
            codes = sbuf(name + "_codes", [P, width], U32)
            scales = sbuf(name + "_scales", [P, width], U8)
            nc.vector.quantize_mx(
                out=codes[0:parts, :].bitcast(FP8X4),
                scales=scales[0:parts, :],
                in_=words[0:parts].rearrange("q c j -> q (c j)"),
            )
            return codes, scales

        def product(bank, g, stat, mov):
            nc.tensor.matmul_mx(
                out=bank[:],
                lhsT=stat[0][rows(g), :].bitcast(FP8X4),
                lhsT_scale=stat[1][rows(g), :],
                rhs=mov[0][rows(g), :].bitcast(FP8X4),
                rhs_scale=mov[1][rows(g), :],
                start=True,
                stop=True,
            )

        x_raw = load_rows("x_raw", x)
        w1_raw = load_rows("w1_raw", w1)
        w2_raw = load_rows("w2_raw", w2)
        wo_raw = load_rows("wo_raw", wo2)
        hs_sb = sbuf("hs_sb", [P, G, 2], F32)
        hs_v = hs.rearrange("g (p h t) one -> h p g (t one)", h=2, t=2)
        for h in range(2):
            nc.sync.dma_start(out=hs_sb[rows(h)], in_=hs_v[h])
        ob_sb = sbuf("ob_sb", [P, G, 2], F32)
        nc.sync.dma_start(out=ob_sb[:], in_=ob.rearrange("g (q t) one -> q g (t one)", t=2))
        osc_sb = sbuf("osc_sb", [P, G, 2], F32)
        nc.sync.dma_start(out=osc_sb[:], in_=osc.rearrange("g (q t) one -> q g (t one)", t=2))

        warm = sbuf("warm", [P, 2], F32)
        nc.vector.memset(warm[:, 0:1], 1.0)
        nc.scalar.activation(out=warm[:, 1:2], in_=warm[:, 0:1], func=ACT.Abs_reciprocal_sqrt)

        ones = sbuf("ones", [P, P * PACK], BF16)
        nc.vector.memset(ones[:].bitcast(I32), 0x3F803F80)
        onesq = (sbuf("ones_codes", [P, N], U32), sbuf("ones_scales", [P, N], U8))
        for c in range(N // P):
            cols = slice(c * P, (c + 1) * P)
            nc.vector.quantize_mx(out=onesq[0][:, cols].bitcast(FP8X4), scales=onesq[1][:, cols], in_=ones[:])
        idle_bank = ps.tile([P, N], F32, name="idle_bank")

        def keep_warm(count, stat):
            for k in range(count):
                nc.tensor.matmul_mx(
                    out=idle_bank[:],
                    lhsT=stat[0][:, 0:P].bitcast(FP8X4),
                    lhsT_scale=stat[1][:, 0:P],
                    rhs=onesq[0][:].bitcast(FP8X4),
                    rhs_scale=onesq[1][:],
                    start=True,
                    stop=True,
                )

        keep_warm(12, onesq)

        x_words = sbuf("x_words", [P, N, PACK], BF16)
        x_dst = x_words[:].rearrange("q (c i) j -> q c j i", i=4)
        x_src = x_raw[:].rearrange("q j (c i) -> q c j i", i=4)
        cs = X_SPLIT // 4
        ch = N // 8
        nc.vector.tensor_copy(out=x_dst[:, 0:ch], in_=x_src[:, 0:ch])
        nc.vector.tensor_copy(out=x_dst[:, ch:cs], in_=x_src[:, ch:cs])
        nc.scalar.copy(out=x_dst[:, cs:], in_=x_src[:, cs:])
        xq = (sbuf("x_codes", [P, N], U32), sbuf("x_scales", [P, N], U8))
        for c in range(2):
            cols = slice(c * (N // 2), (c + 1) * (N // 2))
            nc.vector.quantize_mx(
                out=xq[0][:, cols].bitcast(FP8X4),
                scales=xq[1][:, cols],
                in_=x_words[:, cols, :].rearrange("q c j -> q (c j)"),
            )

        keep_warm(1, xq)

        def deal(name, raw, t, copy):
            words = sbuf(name + "_words", [P, P, PACK], BF16)
            copy(
                out=words[:].rearrange("q (h p) j -> q p h j", h=2),
                in_=raw[:].rearrange("q j (p h t) -> q t p h j", t=2, h=2)[:, t],
            )
            return words

        z1 = [[ps.tile([P, N], F32, name="z1_%d%d" % (g, t)) for t in range(2)] for g in range(G)]
        z2_1 = ps.tile([P, N], F32, name="z2_1")
        z2 = [[ps.tile([P, N], F32, name="z2_0%d" % t) for t in range(2)], [z2_1, z2_1]]

        w10 = deal("w10", w1_raw, 0, nc.scalar.copy)
        w11 = deal("w11", w1_raw, 1, nc.vector.tensor_copy)
        w1q0 = quantize("w10", w10, P)
        product(z1[0][0], 0, w1q0, xq)
        product(z1[1][0], 1, w1q0, xq)
        w20 = deal("w20", w2_raw, 0, nc.vector.tensor_copy)
        w21 = deal("w21", w2_raw, 1, nc.scalar.copy)
        w1q1 = quantize("w11", w11, P)
        w2q0 = quantize("w20", w20, P)
        w2q1 = quantize("w21", w21, P)
        product(z2[0][0], 0, w2q0, xq)
        product(z1[0][1], 0, w1q1, xq)
        product(z2[1][0], 1, w2q0, xq)
        product(z2[0][1], 0, w2q1, xq)
        product(z1[1][1], 1, w1q1, xq)


        squares = sbuf("squares", [P, N], BF16)
        sumsq = [sbuf("sumsq%d" % g, [P, 2], F32) for g in range(G)]
        rs = [sbuf("rs%d" % g, [P, 2], F32) for g in range(G)]
        fac = [sbuf("fac%d" % g, [P, 2], F32) for g in range(G)]
        sumpr = [[sbuf("sumpr%d%d" % (g, t), [P, 1], F32) for t in range(2)] for g in range(G)]
        mu = [[sbuf("mu%d%d" % (g, t), [P, 1], F32) for t in range(2)] for g in range(G)]
        z1_sb = [[sbuf("z1_sb%d%d" % (g, t), [P, N], F32) for t in range(2)] for g in range(G)]
        pr = [[sbuf("pr%d%d" % (g, t), [P, N], F32) for t in range(2)] for g in range(G)]

        def square(g, t):
            nc.scalar.activation(
                out=squares[:], in_=z1[g][t][:], func=ACT.Square, accum_out=sumsq[g][:, t : t + 1]
            )

        def root(g):
            nc.scalar.activation(
                out=rs[g][:], in_=sumsq[g][:], func=ACT.Abs_reciprocal_sqrt, scale=1.0 / N, bias=EPS
            )

        def multiply(g, t):
            nc.vector.scalar_tensor_tensor(
                out=pr[g][t][:], in0=z2[g][t][:], scalar=1.0, in1=z1_sb[g][t][:],
                op0=ALU.mult, op1=ALU.mult, accum_out=sumpr[g][t][:],
            )

        def mean(g, t):
            nc.vector.tensor_scalar(
                out=mu[g][t][:], in0=sumpr[g][t][:], scalar1=1.0 / N, scalar2=None, op0=ALU.mult
            )

        def factor(g):
            nc.vector.tensor_tensor(out=fac[g][:], in0=rs[g][:], in1=hs_sb[:, g, :], op=ALU.mult)

        def centre(g, t, pair, cols):
            nc.vector.tensor_scalar(
                out=pair[:, g, :, t], in0=pr[g][t][:, cols], scalar1=mu[g][t][:],
                scalar2=fac[g][:, t : t + 1], op0=ALU.subtract, op1=ALU.mult,
            )

        def swap(g, pair):
            pw = pair[:].rearrange("q h n t -> q h (n t)").bitcast(I32)
            nc.sync.dma_start(out=pw[rows(g), 1 - g, :], in_=pw[rows(1 - g), g, :])
            return pw

        H = N // 2
        halves = [slice(0, H), slice(H, N)]
        pair0 = sbuf("pair0", [P, 2, N, 2], BF16)
        pair1 = [sbuf("pair1%d" % c, [P, 2, H, 2], BF16) for c in range(2)]

        nc.scalar.copy(out=z1_sb[0][0][:], in_=z1[0][0][:])
        nc.vector.tensor_copy(out=z1_sb[1][0][:], in_=z1[1][0][:])
        square(0, 0)
        multiply(0, 0)
        nc.scalar.copy(out=z1_sb[0][1][:], in_=z1[0][1][:])
        square(0, 1)
        root(0)
        multiply(1, 0)
        product(z2[1][1], 1, w2q1, xq)
        mean(0, 0)
        multiply(0, 1)
        product(z2[0][1], 0, w2q1, xq)
        keep_warm(3, onesq)
        mean(1, 0)
        factor(0)
        mean(0, 1)
        centre(0, 0, pair0, slice(0, N))
        centre(0, 1, pair0, slice(0, N))
        pw0 = swap(0, pair0)
        nc.scalar.copy(out=z1_sb[1][1][:], in_=z1[1][1][:])
        square(1, 0)
        square(1, 1)
        root(1)
        multiply(1, 1)
        product(z2[1][1], 1, w2q1, xq)
        keep_warm(6, onesq)
        factor(1)
        mean(1, 1)
        pw1 = []
        for c in range(2):
            for t in range(2):
                centre(1, t, pair1[c], halves[c])
            pw1.append(swap(1, pair1[c]))

        wo_words = sbuf("wo_words", [P, O, PACK], BF16)
        nc.scalar.copy(
            out=wo_words[:].rearrange("q (t p) j -> q p t j", t=2),
            in_=wo_raw[:].rearrange("q j (p t) -> q p t j", t=2),
        )

        nc.scalar.activation(out=warm[:, 1:2], in_=warm[:, 0:1], func=ACT.Tanh)

        h_words = sbuf("h_words", [P, N, PACK], BF16)
        hw = h_words[:].rearrange("q n j -> q (n j)").bitcast(I32)
        out_v = out.rearrange("g (q t) n -> g t q n", t=2)

        def join(g, pw, cols):
            nc.vector.tensor_copy(
                out=hw[rows(g), 2 * cols.start : 2 * cols.stop].rearrange("q (c i h) -> q c h i", i=4, h=2),
                in_=pw[rows(g)].rearrange("q h (c i) -> q c h i", i=4),
            )

        join(0, pw0, slice(0, N))
        wo_codes, wo_scales = quantize("wo", wo_words, P)
        woq = [(wo_codes[:, P * t : P * (t + 1)], wo_scales[:, P * t : P * (t + 1)]) for t in range(2)]
        keep_warm(2, (wo_codes, wo_scales))
        hq0 = quantize("h0", h_words, R)
        for t in range(2):
            product(z1[0][t], 0, woq[t], hq0)
        keep_warm(2, onesq)
        h1_codes = sbuf("h1_codes", [P, N], U32)
        h1_scales = sbuf("h1_scales", [P, N], U8)
        for c in range(2):
            join(1, pw1[c], halves[c])
        for c in range(2):
            nc.vector.quantize_mx(
                out=h1_codes[:, halves[c]].bitcast(FP8X4),
                scales=h1_scales[:, halves[c]],
                in_=h_words[:, halves[c], :].rearrange("q c j -> q (c j)"),
            )
        for t in range(2):
            product(z1[1][t], 1, woq[t], (h1_codes, h1_scales))
        for g in range(G):
            for t in range(2):
                chunks = 2 if (g, t) == (1, 1) else 1
                width = N // chunks
                for c in range(chunks):
                    cols = slice(c * width, (c + 1) * width)
                    th = sbuf("th%d%d%d" % (g, t, c), [P, width], F32)
                    nc.scalar.activation(
                        out=th[:], in_=z1[g][t][:, cols], func=ACT.Tanh, bias=ob_sb[:, g, t : t + 1]
                    )
                    res = sbuf("res%d%d%d" % (g, t, c), [P, width], F32)
                    nc.vector.tensor_scalar(
                        out=res[:], in0=th[:], scalar1=osc_sb[:, g, t : t + 1], scalar2=None, op0=ALU.mult
                    )
                    nc.sync.dma_start(out=out_v[g, t][:, cols], in_=res[:])
